import numpy as np
import ml_dtypes


def mxq(x, axis, fmt="e4m3"):
    dtype, down = {"e4m3": (ml_dtypes.float8_e4m3fn, 7), "e5m2": (ml_dtypes.float8_e5m2, 14)}[fmt]
    v = np.moveaxis(np.asarray(x, np.float32).astype(ml_dtypes.bfloat16).astype(np.float64), axis, -1)
    blocks = v.reshape(v.shape[:-1] + (-1, 32))
    amax = np.abs(blocks).max(-1, keepdims=True)
    byte = np.maximum(np.where(amax > 0, np.frexp(amax)[1] - 1 + 127, 0) - down, 1)
    scale = np.exp2(byte - 127.0)
    codes = (blocks / scale).astype(np.float32).astype(dtype).astype(np.float64)
    return np.moveaxis((codes * scale).reshape(v.shape), -1, axis)


WIDE = False


def mx_kscale(k):
    if not WIDE:
        return np.ones(k)
    levels = np.array([30, -30])
    if k % 512:
        return np.exp2(np.random.permutation(np.resize(levels, k // 32))).repeat(32)
    a = np.empty((k // 512, 16))
    for p in range(k // 512):
        a[p, :8] = np.random.permutation(np.resize(levels, 8))
        for g in range(8):
            far = levels[np.abs(levels - a[p, g]) >= 10]
            a[p, g + 8] = far[np.random.randint(len(far))]
    return np.exp2(a.ravel()).repeat(32)


def f64(x):
    return np.asarray(x).astype(np.float64)


def striped(idx):
    return np.tile(np.asarray(idx).reshape(-1, 16).T, (8, 1)).astype(np.uint16)


def unstriped(offs):
    return offs[:16].T.reshape(-1).astype(np.int64)


def striped8(idx):
    return np.asarray(idx).reshape(8, -1, 16).transpose(0, 2, 1).reshape(128, -1).astype(np.uint16)


def unstriped8(offs):
    return offs.reshape(8, 16, -1).transpose(0, 2, 1).reshape(8, -1).astype(np.int64)


def pick8(x, idx, run):
    r = np.arange(len(x))
    return x[r[:, None], idx[r % (8 * run) // run]]


E2M1 = np.array([0.0, 0.5, 1.0, 1.5, 2.0, 3.0, 4.0, 6.0, -0.0, -0.5, -1.0, -1.5, -2.0, -3.0, -4.0, -6.0])


def pack_weight(w, fmt):
    k, n = w.shape
    w = f64(np.asarray(w, np.float32).astype(ml_dtypes.bfloat16)).reshape(k // 32, 32, n)
    amax = np.abs(w).max(1)
    if fmt in ("e4m3", "e5m2"):
        byte = np.frexp(amax)[1] - 1 + 127 - (7 if fmt == "e4m3" else 14)
    else:
        mant, ex = np.frexp(amax / 6.0)
        byte = np.where(mant > 0.5, ex, ex - 1) + 127
    byte = np.clip(np.where(amax > 0, byte, 1), 1, 254)
    scaled = (w * np.exp2(127.0 - byte)[:, None, :]).reshape(k, n).astype(np.float32)
    by_word = np.ascontiguousarray(scaled.reshape(k // 512, 128, 4, n).transpose(0, 1, 3, 2))
    if fmt in ("e4m3", "e5m2"):
        words = by_word.astype(ml_dtypes.float8_e4m3fn if fmt == "e4m3" else ml_dtypes.float8_e5m2).view(np.uint8)
    else:
        c = by_word.astype(ml_dtypes.float4_e2m1fn).view(np.uint8) & 0xF
        words = (c[..., 0::2] | (c[..., 1::2] << 4)).reshape(k // 512, 128, 2 * n)
    return np.ascontiguousarray(words), np.ascontiguousarray(byte.astype(np.uint8).reshape(k // 512, 16, n))


def unpack_weight(words, scales, fmt):
    g, _, n = scales.shape
    words = np.ascontiguousarray(words).reshape(g, 128, n, -1)
    if fmt in ("e4m3", "e5m2"):
        vals = words.view(ml_dtypes.float8_e4m3fn if fmt == "e4m3" else ml_dtypes.float8_e5m2).astype(np.float64)
    else:
        nib = np.empty((g, 128, n, 4), np.uint8)
        nib[..., 0::2] = words & 0xF
        nib[..., 1::2] = words >> 4
        vals = E2M1[nib]
    vals = vals * np.repeat(np.exp2(scales.astype(np.float64) - 127.0), 8, axis=1)[..., None]
    return vals.transpose(0, 1, 3, 2).reshape(g * 512, n)


K, T, J, R, F, Z, C, O, N, E = 512, 1024, 256, 512, 512, 1024, 512, 128, 256, 1024


def setup_inputs():
    n = np.random.standard_normal
    idx = np.random.permutation(T)[:J]
    idx2 = np.random.permutation(Z)[:J]
    idx3 = np.stack([np.random.permutation(C)[:J] for _ in range(8)])
    idx4 = np.random.permutation(C)[:O]
    idx5 = np.random.permutation(C)[:O]
    idx6 = np.random.permutation(J)[:O]
    idx7 = np.random.permutation(E)[:O]
    fk = mx_kscale(K)
    ff = mx_kscale(F)
    fr = mx_kscale(R)
    xtp = pack_weight(n((K, T)) / fk[:, None], "e2m1")
    xop = pack_weight(n((F, Z)) / ff[:, None], "e4m3")
    wp = pack_weight(n((K, R)) * 1 / np.sqrt(K) * fk[:, None] * fr, "e4m3")
    w2p = pack_weight(n((K, R)) * 1 / np.sqrt(K) * fk[:, None] * fr, "e5m2")
    w0p = pack_weight(n((F, R)) * 1 / np.sqrt(F) * ff[:, None] * fr, "e5m2")
    wbp = pack_weight(n((R, N)) * 1 / np.sqrt(R) / fr[:, None], "e2m1")
    return {
        "xt_words": xtp[0],
        "xt_scales": xtp[1],
        "xo_words": xop[0],
        "xo_scales": xop[1],
        "w_words": wp[0],
        "w_scales": wp[1],
        "w2_words": w2p[0],
        "w2_scales": w2p[1],
        "w0_words": w0p[0],
        "w0_scales": w0p[1],
        "sa": (np.random.uniform(0.5, 1.6, (R, 1))).astype(np.float32),
        "sb": (np.random.uniform(0.5, 1.6, (R, 1))).astype(np.float32),
        "sd": (np.random.uniform(0.5, 1.6, (R, 1))).astype(np.float32),
        "wb_words": wbp[0],
        "wb_scales": wbp[1],
        "offs": striped(idx),
        "offs2": striped(idx2),
        "offs3": striped8(idx3),
        "offs4": striped(idx4),
        "offs5": striped(idx5),
        "offs6": striped(idx6),
        "offs7": striped(idx7),
    }


def reference(xt_words, xt_scales, xo_words, xo_scales, w_words, w_scales, w2_words, w2_scales, w0_words, w0_scales, sa, sb, sd, wb_words, wb_scales, offs, offs2, offs3, offs4, offs5, offs6, offs7):
    idx = unstriped(offs)
    idx2 = unstriped(offs2)
    idx3 = unstriped8(offs3)
    idx4 = unstriped(offs4)
    idx5 = unstriped(offs5)
    idx6 = unstriped(offs6)
    idx7 = unstriped(offs7)
    xtu = unpack_weight(xt_words, xt_scales, "e2m1")
    xou = unpack_weight(xo_words, xo_scales, "e4m3")
    wu = unpack_weight(w_words, w_scales, "e4m3")
    w2u = unpack_weight(w2_words, w2_scales, "e5m2")
    w0u = unpack_weight(w0_words, w0_scales, "e5m2")
    wbu = unpack_weight(wb_words, wb_scales, "e2m1")
    xtidxg = xtu[:, idx]
    a = wu.T @ xtidxg
    xoidx2g = xou[:, idx2]
    b = w2u.T @ xtidxg + w0u.T @ xoidx2g
    pw = np.zeros((R, C))
    pw[np.arange(R)[:, None], idx3[np.arange(R) % 512 // 64]] = a
    hid = np.maximum(pw[:, idx4] * f64(sa), pw[:, idx5] * f64(sb)) - b[:, idx6] * f64(sd)
    hidq = mxq(hid, 0, "e5m2")
    p = wbu.T @ hidq
    y = np.zeros((N, E))
    y[:, idx7] = p
    return y

@@ -1,0 +1,220 @@
+from contextlib import ExitStack
+
+import concourse.mybir as mybir
+
+F32 = mybir.dt.float32
+BF16 = mybir.dt.bfloat16
+I32 = mybir.dt.int32
+U32 = mybir.dt.uint32
+U16 = mybir.dt.uint16
+U8 = mybir.dt.uint8
+E4M3 = mybir.dt.float8_e4m3fn_x4
+E5M2 = mybir.dt.float8_e5m2_x4
+E2M1 = mybir.dt.float4_e2m1fn_x4
+COPY = mybir.ActivationFunctionType.Copy
+ALU = mybir.AluOpType
+
+P = 128
+PACK = 4
+T, J, R, Z, C, O, N, E = 1024, 256, 512, 1024, 512, 128, 256, 1024
+HALF = J // 2
+
+FLOPS = 2 * 512 * R * J * 3 + 2 * R * N * O
+
+
+def tile_list_ownthree_leaned_one_scattered_kernel(
+    tc, xt_words, xt_scales, xo_words, xo_scales, w_words, w_scales, w2_words, w2_scales,
+    w0_words, w0_scales, sa, sb, sd, wb_words, wb_scales,
+    offs, offs2, offs3, offs4, offs5, offs6, offs7, out,
+):
+    nc = tc.nc
+    with ExitStack() as ctx:
+        lists = ctx.enter_context(tc.tile_pool(name="lists", bufs=1))
+        keep = ctx.enter_context(tc.tile_pool(name="keep", bufs=1))
+        psum = ctx.enter_context(tc.psum_pool(name="psum", bufs=1))
+
+        def load_list(src, name):
+            tile = lists.tile(list(src.shape), U16, name=name)
+            nc.sync.dma_start(tile[:], src)
+            return tile
+
+        def load_scale_rows(queue, dst, src):
+            queue.dma_start(dst, src[0].bitcast(I32).rearrange("(q r) n -> r q n", r=4))
+
+        def spread_scale_rows(plane, staged):
+            for q in range(4):
+                nc.vector.tensor_copy(out=plane[32 * q : 32 * q + 4, :].bitcast(I32), in_=staged[:, q, :])
+
+        def load_words(queue, dst, src):
+            queue.dma_start(dst.bitcast(I32), src.bitcast(I32))
+
+        def deal(dst, src, run, ts=slice(0, PACK)):
+            nc.vector.tensor_copy(
+                out=dst.rearrange("p (t c i) -> p c t i", t=PACK, i=run)[:, :, ts, :],
+                in_=src.rearrange("p (c i t) -> p c t i", t=PACK, i=run)[:, :, ts, :],
+            )
+
+        w_stage = keep.tile([4, 4, R // 4], I32, name="w_stage")
+        xt_plane = keep.tile([P, T], U8, name="xt_plane", align_bytes=64)
+        xo_plane = keep.tile([P, Z], U8, name="xo_plane", align_bytes=64)
+        w_plane = keep.tile([P, R], U8, name="w_plane", align_bytes=64)
+        late_plane = keep.tile([P, 2 * R + N], U8, name="late_plane", align_bytes=64)
+        xt_tab = keep.tile([P, T], U16, name="xt_tab", tag="board3", align_bytes=64)
+        xo_tab = keep.tile([P, Z], U32, name="xo_tab", align_bytes=64)
+        w_raw = keep.tile([P, R], I32, name="w_raw", tag="board2", align_bytes=64)
+        w2_raw = keep.tile([P, R], I32, name="w2_raw", align_bytes=64)
+        w0_raw = keep.tile([P, R], I32, name="w0_raw", align_bytes=64)
+        wb_codes = keep.tile([P, 2 * N], U8, name="wb_codes", align_bytes=64)
+        sa_t = keep.tile([P, PACK], F32, name="sa_t")
+        sb_t = keep.tile([P, PACK], F32, name="sb_t")
+        sd_t = keep.tile([P, PACK], F32, name="sd_t")
+
+        boards = [keep.tile([P, C], F32, name=f"board{t}") for t in range(2)]
+        for plane in (xt_plane, w_plane, xo_plane, late_plane):
+            nc.vector.memset(plane[:].bitcast(I32), 0)
+        for board in boards:
+            nc.vector.memset(board[:], 0.0)
+
+        def load_plane(dst, src, queues=(nc.sync,) * 4):
+            for q in range(4):
+                queues[q].dma_start(dst[32 * q : 32 * q + 4, :].bitcast(I32), src[0, 4 * q : 4 * q + 4, :].bitcast(I32))
+
+        l1 = load_list(offs, "l1")
+        load_scale_rows(nc.scalar, w_stage[:], w_scales)
+        load_plane(xt_plane[:], xt_scales, (nc.sync, nc.scalar, nc.sync, nc.scalar))
+        load_words(nc.sync, xt_tab[:], xt_words[0])
+        load_words(nc.scalar, w_raw[:], w_words[0].rearrange("p n t -> p (n t)"))
+        l3 = load_list(offs3, "l3")
+
+        def load_weights(dst, src):
+            nc.sync.dma_start(dst[:], src.rearrange("(p t) one -> p (t one)", t=PACK))
+
+        l2 = load_list(offs2, "l2")
+        load_words(nc.sync, xo_tab[:], xo_words[0].rearrange("p n t -> p (n t)"))
+        load_plane(xo_plane[:], xo_scales)
+        load_plane(late_plane[:, 0:R], w2_scales)
+        load_plane(late_plane[:, R : 2 * R], w0_scales)
+        load_words(nc.sync, w2_raw[:], w2_words[0].rearrange("p n t -> p (n t)"))
+        load_words(nc.sync, w0_raw[:], w0_words[0].rearrange("p n t -> p (n t)"))
+        l4 = load_list(offs4, "l4")
+        load_weights(sa_t, sa)
+        l5 = load_list(offs5, "l5")
+        load_weights(sb_t, sb)
+        l6 = load_list(offs6, "l6")
+        load_weights(sd_t, sd)
+        load_plane(late_plane[:, 2 * R :], wb_scales)
+        load_words(nc.sync, wb_codes[:], wb_words[0])
+        l7 = load_list(offs7, "l7")
+
+        spread_scale_rows(w_plane, w_stage)
+        xt_gw = keep.tile([P, J], U16, name="xt_gw", align_bytes=64)
+        xt_gs = keep.tile([P, J], U8, name="xt_gs", align_bytes=64)
+        w_sc = keep.tile([P, R], U8, name="w_sc", align_bytes=64)
+        w_cd = keep.tile([P, R], I32, name="w_cd", align_bytes=64)
+        halves = [slice(0, HALF), slice(HALF, J)]
+        lhalves = [slice(0, HALF // 16), slice(HALF // 16, J // 16)]
+        deal(w_sc[:], w_plane[:], 16, slice(0, 2))
+        nc.vector.tensor_copy(xt_gs[:, halves[0]], xt_plane[:].indirect(l1[:, lhalves[0]]))
+        nc.vector.tensor_copy(xt_gw[:, halves[0]], xt_tab[:].indirect(l1[:, lhalves[0]]))
+        deal(w_cd[:], w_raw[:], 4, slice(0, 2))
+
+        def product(dst, codes, fmt, scales, t, xw, xfmt, xs, cols, start, stop):
+            rows = slice(P * t, P * (t + 1))
+            nc.tensor.matmul_mx(
+                out=dst, lhsT=codes[:, rows].bitcast(fmt), lhsT_scale=scales[:, rows],
+                rhs=xw[:, cols].bitcast(xfmt), rhs_scale=xs[:, cols], start=start, stop=stop,
+            )
+
+        a_sb = [keep.tile([P, J], F32, name=f"a_sb{t}") for t in range(PACK)]
+        a_first = [psum.tile([P, HALF], F32, name=f"a_first{t}") for t in range(2)]
+        a_second = psum.tile([P, 2, HALF], F32, name="a_second")
+        a_whole = psum.tile([P, 2, J], F32, name="a_whole")
+        for t in range(2):
+            product(a_first[t][:], w_cd, E4M3, w_sc, t, xt_gw, E2M1, xt_gs, halves[0], True, True)
+        nc.scalar.activation(a_sb[0][:, halves[0]], a_first[0][:], COPY)
+        nc.scalar.activation(boards[0][:].indirect(l3[:, lhalves[0]]), a_sb[0][:, halves[0]], COPY)
+
+        nc.vector.tensor_copy(xt_gs[:, halves[1]], xt_plane[:].indirect(l1[:, lhalves[1]]))
+        nc.vector.tensor_copy(xt_gw[:, halves[1]], xt_tab[:].indirect(l1[:, lhalves[1]]))
+        nc.vector.tensor_copy(a_sb[1][:, halves[0]], a_first[1][:])
+        nc.scalar.activation(boards[1][:].indirect(l3[:, lhalves[0]]), a_sb[1][:, halves[0]], COPY)
+        for t in range(2):
+            product(a_second[:, t, :], w_cd, E4M3, w_sc, t, xt_gw, E2M1, xt_gs, halves[1], True, True)
+        deal(w_sc[:], w_plane[:], 16, slice(2, PACK))
+        deal(w_cd[:], w_raw[:], 4, slice(2, PACK))
+        for t in range(2):
+            product(a_whole[:, t, :], w_cd, E4M3, w_sc, 2 + t, xt_gw, E2M1, xt_gs, slice(0, J), True, True)
+        for t in range(2):
+            nc.vector.tensor_copy(a_sb[t][:, halves[1]], a_second[:, t, :])
+        for t in range(2):
+            nc.scalar.activation(boards[t][:].indirect(l3[:, lhalves[1]]), a_sb[t][:, halves[1]], COPY)
+        for t in range(2, PACK):
+            board = keep.tile([P, C], F32, name=f"board{t}", tag=f"board{t}", align_bytes=64)
+            nc.vector.memset(board[:], 0.0)
+            boards.append(board)
+            nc.vector.tensor_copy(a_sb[t][:], a_whole[:, t - 2, :])
+            nc.scalar.activation(boards[t][:].indirect(l3[:]), a_sb[t][:], COPY)
+
+        xo_gw = keep.tile([P, J], U32, name="xo_gw", align_bytes=64)
+        xo_gs = keep.tile([P, J], U8, name="xo_gs", align_bytes=64)
+        w2_sc = keep.tile([P, R], U8, name="w2_sc", align_bytes=64)
+        w0_sc = keep.tile([P, R], U8, name="w0_sc", align_bytes=64)
+        w2_cd = keep.tile([P, R], I32, name="w2_cd", tag="page0", align_bytes=64)
+        w0_cd = keep.tile([P, R], I32, name="w0_cd", tag="page1", align_bytes=64)
+        nc.vector.tensor_copy(xo_gw[:], xo_tab[:].indirect(l2[:]))
+        nc.vector.tensor_copy(xo_gs[:], xo_plane[:].indirect(l2[:]))
+        deal(w2_sc[:], late_plane[:, 0:R], 16)
+        deal(w0_sc[:], late_plane[:, R : 2 * R], 16)
+        deal(w2_cd[:], w2_raw[:], 4)
+        deal(w0_cd[:], w0_raw[:], 4)
+        b_ps = [psum.tile([P, 2, J], F32, name=f"b_ps{u}") for u in range(2)]
+        b_sb = [keep.tile([P, J], F32, name=f"b_sb{t}") for t in range(PACK)]
+        for t in range(PACK):
+            dst = b_ps[t // 2][:, t % 2, :]
+            product(dst, w2_cd, E5M2, w2_sc, t, xt_gw, E2M1, xt_gs, slice(0, J), True, False)
+            product(dst, w0_cd, E5M2, w0_sc, t, xo_gw, E4M3, xo_gs, slice(0, J), False, True)
+        for t in range(PACK):
+            nc.vector.tensor_copy(b_sb[t][:], b_ps[t // 2][:, t % 2, :])
+
+        hid = keep.tile([P, O, PACK], BF16, name="hid", align_bytes=64)
+        first = keep.tile([P, PACK, O], F32, name="first")
+        second = keep.tile([P, PACK, O], F32, name="second")
+        third = keep.tile([P, PACK, O], F32, name="third")
+        larger = keep.tile([P, PACK, O], F32, name="larger")
+        for t in range(PACK):
+            nc.scalar.activation(first[:, t, :], boards[t][:].indirect(l4[:]), COPY, scale=sa_t[:, t : t + 1])
+        for t in range(PACK):
+            nc.scalar.activation(second[:, t, :], boards[t][:].indirect(l5[:]), COPY, scale=sb_t[:, t : t + 1])
+        for t in range(PACK):
+            nc.scalar.activation(third[:, t, :], b_sb[t][:].indirect(l6[:]), COPY, scale=sd_t[:, t : t + 1])
+        nc.vector.tensor_tensor(larger[:], first[:], second[:], ALU.max)
+        nc.vector.tensor_tensor(
+            hid[:].rearrange("p (c i) t -> p c t i", i=4),
+            larger[:].rearrange("p t (c i) -> p c t i", i=4),
+            third[:].rearrange("p t (c i) -> p c t i", i=4),
+            ALU.subtract,
+        )
+
+        pages = [keep.tile([P, E], F32, name=f"page{u}", tag=f"page{u}", align_bytes=64) for u in range(2)]
+        for page in pages:
+            nc.vector.memset(page[:], 0.0)
+
+        hid_cd = keep.tile([P, O], U32, name="hid_cd", align_bytes=64)
+        hid_sc = keep.tile([P, O], U8, name="hid_sc", align_bytes=64)
+        nc.vector.quantize_mx(out=hid_cd[:].bitcast(E5M2), scales=hid_sc[:], in_=hid[:].rearrange("p o t -> p (o t)"))
+
+        p_ps = [psum.tile([P, O], F32, name=f"p_ps{u}") for u in range(2)]
+        p_sb = [keep.tile([P, O], F32, name=f"p_sb{u}") for u in range(2)]
+        for u in range(2):
+            nc.tensor.matmul_mx(
+                out=p_ps[u][:],
+                lhsT=wb_codes[:, 2 * P * u : 2 * P * (u + 1)].bitcast(E2M1),
+                lhsT_scale=late_plane[:, 2 * R + P * u : 2 * R + P * (u + 1)],
+                rhs=hid_cd[:].bitcast(E5M2), rhs_scale=hid_sc[:], start=True, stop=True,
+            )
+        nc.vector.tensor_copy(p_sb[0][:], p_ps[0][:])
+        nc.vector.tensor_copy(pages[0][:].indirect(l7[:]), p_sb[0][:])
+        nc.sync.dma_start(out[0:P, :], pages[0][:])
+        nc.scalar.activation(p_sb[1][:], p_ps[1][:], COPY)
+        nc.scalar.activation(pages[1][:].indirect(l7[:]), p_sb[1][:], COPY)
+        nc.scalar.dma_start(out[P : 2 * P, :], pages[1][:])

@@ -31,6 +31,7 @@ def tile_list_ownthree_leaned_one_scattered_kernel(
     with ExitStack() as ctx:
         lists = ctx.enter_context(tc.tile_pool(name="lists", bufs=1))
         keep = ctx.enter_context(tc.tile_pool(name="keep", bufs=1))
+        shared = ctx.enter_context(tc.tile_pool(name="shared", bufs=1))
         psum = ctx.enter_context(tc.psum_pool(name="psum", bufs=1))
 
         def load_list(src, name):
@@ -48,20 +49,21 @@ def tile_list_ownthree_leaned_one_scattered_kernel(
         def load_words(queue, dst, src):
             queue.dma_start(dst.bitcast(I32), src.bitcast(I32))
 
-        def deal(dst, src, run, ts=slice(0, PACK)):
+        def deal(dst, src, run):
             nc.vector.tensor_copy(
-                out=dst.rearrange("p (t c i) -> p c t i", t=PACK, i=run)[:, :, ts, :],
-                in_=src.rearrange("p (c i t) -> p c t i", t=PACK, i=run)[:, :, ts, :],
+                out=dst.rearrange("p (t c i) -> p c t i", t=PACK, i=run),
+                in_=src.rearrange("p (c i t) -> p c t i", t=PACK, i=run),
             )
 
         w_stage = keep.tile([4, 4, R // 4], I32, name="w_stage")
+        late_stage = keep.tile([4, 4, (2 * R + N) // 4], I32, name="late_stage")
         xt_plane = keep.tile([P, T], U8, name="xt_plane", align_bytes=64)
         xo_plane = keep.tile([P, Z], U8, name="xo_plane", align_bytes=64)
         w_plane = keep.tile([P, R], U8, name="w_plane", align_bytes=64)
         late_plane = keep.tile([P, 2 * R + N], U8, name="late_plane", align_bytes=64)
         xt_tab = keep.tile([P, T], U16, name="xt_tab", tag="board3", align_bytes=64)
         xo_tab = keep.tile([P, Z], U32, name="xo_tab", align_bytes=64)
-        w_raw = keep.tile([P, R], I32, name="w_raw", tag="board2", align_bytes=64)
+        w_raw = shared.tile([P, R], I32, name="w_raw", align_bytes=64, offset=0)
         w2_raw = keep.tile([P, R], I32, name="w2_raw", align_bytes=64)
         w0_raw = keep.tile([P, R], I32, name="w0_raw", align_bytes=64)
         wb_codes = keep.tile([P, 2 * N], U8, name="wb_codes", align_bytes=64)
@@ -81,8 +83,8 @@ def tile_list_ownthree_leaned_one_scattered_kernel(
 
         l1 = load_list(offs, "l1")
         load_scale_rows(nc.scalar, w_stage[:], w_scales)
-        load_plane(xt_plane[:], xt_scales, (nc.sync, nc.scalar, nc.sync, nc.scalar))
         load_words(nc.sync, xt_tab[:], xt_words[0])
+        load_plane(xt_plane[:], xt_scales, (nc.scalar, nc.sync, nc.scalar, nc.sync))
         load_words(nc.scalar, w_raw[:], w_words[0].rearrange("p n t -> p (n t)"))
         l3 = load_list(offs3, "l3")
 
@@ -92,66 +94,67 @@ def tile_list_ownthree_leaned_one_scattered_kernel(
         l2 = load_list(offs2, "l2")
         load_words(nc.sync, xo_tab[:], xo_words[0].rearrange("p n t -> p (n t)"))
         load_plane(xo_plane[:], xo_scales)
-        load_plane(late_plane[:, 0:R], w2_scales)
-        load_plane(late_plane[:, R : 2 * R], w0_scales)
-        load_words(nc.sync, w2_raw[:], w2_words[0].rearrange("p n t -> p (n t)"))
+        load_scale_rows(nc.sync, late_stage[:, :, 0 : R // 4], w2_scales)
+        load_scale_rows(nc.sync, late_stage[:, :, R // 4 : 2 * R // 4], w0_scales)
+        load_scale_rows(nc.sync, late_stage[:, :, 2 * R // 4 :], wb_scales)
         load_words(nc.sync, w0_raw[:], w0_words[0].rearrange("p n t -> p (n t)"))
+        load_words(nc.sync, w2_raw[:], w2_words[0].rearrange("p n t -> p (n t)"))
         l4 = load_list(offs4, "l4")
         load_weights(sa_t, sa)
         l5 = load_list(offs5, "l5")
         load_weights(sb_t, sb)
         l6 = load_list(offs6, "l6")
         load_weights(sd_t, sd)
-        load_plane(late_plane[:, 2 * R :], wb_scales)
         load_words(nc.sync, wb_codes[:], wb_words[0])
         l7 = load_list(offs7, "l7")
 
-        spread_scale_rows(w_plane, w_stage)
-        xt_gw = keep.tile([P, J], U16, name="xt_gw", align_bytes=64)
-        xt_gs = keep.tile([P, J], U8, name="xt_gs", align_bytes=64)
-        w_sc = keep.tile([P, R], U8, name="w_sc", align_bytes=64)
-        w_cd = keep.tile([P, R], I32, name="w_cd", align_bytes=64)
         halves = [slice(0, HALF), slice(HALF, J)]
         lhalves = [slice(0, HALF // 16), slice(HALF // 16, J // 16)]
-        deal(w_sc[:], w_plane[:], 16, slice(0, 2))
-        nc.vector.tensor_copy(xt_gs[:, halves[0]], xt_plane[:].indirect(l1[:, lhalves[0]]))
-        nc.vector.tensor_copy(xt_gw[:, halves[0]], xt_tab[:].indirect(l1[:, lhalves[0]]))
-        deal(w_cd[:], w_raw[:], 4, slice(0, 2))
+        w_sc = keep.tile([P, R], U8, name="w_sc", align_bytes=64)
+        w_cd = keep.tile([P, R], I32, name="w_cd", align_bytes=64)
+        xt_gs = [keep.tile([P, HALF], U8, name="xt_gs0", align_bytes=64)]
+        xt_gw = [keep.tile([P, HALF], U16, name="xt_gw0", align_bytes=64)]
+        spread_scale_rows(w_plane, w_stage)
+        deal(w_sc[:], w_plane[:], 16)
+        nc.vector.tensor_copy(xt_gw[0][:], xt_tab[:].indirect(l1[:, lhalves[0]]))
+        nc.vector.tensor_copy(xt_gs[0][:], xt_plane[:].indirect(l1[:, lhalves[0]]))
+        deal(w_cd[:], w_raw[:], 4)
 
-        def product(dst, codes, fmt, scales, t, xw, xfmt, xs, cols, start, stop):
+        def product(dst, codes, fmt, scales, t, xw, xfmt, xs, start, stop):
             rows = slice(P * t, P * (t + 1))
             nc.tensor.matmul_mx(
                 out=dst, lhsT=codes[:, rows].bitcast(fmt), lhsT_scale=scales[:, rows],
-                rhs=xw[:, cols].bitcast(xfmt), rhs_scale=xs[:, cols], start=start, stop=stop,
+                rhs=xw[:].bitcast(xfmt), rhs_scale=xs[:], start=start, stop=stop,
             )
 
         a_sb = [keep.tile([P, J], F32, name=f"a_sb{t}") for t in range(PACK)]
-        a_first = [psum.tile([P, HALF], F32, name=f"a_first{t}") for t in range(2)]
+        a_first = [psum.tile([P, HALF], F32, name=f"a_first{t}", tag=f"small{t}") for t in range(2)]
         a_second = psum.tile([P, 2, HALF], F32, name="a_second")
         a_whole = psum.tile([P, 2, J], F32, name="a_whole")
         for t in range(2):
-            product(a_first[t][:], w_cd, E4M3, w_sc, t, xt_gw, E2M1, xt_gs, halves[0], True, True)
+            product(a_first[t][:], w_cd, E4M3, w_sc, t, xt_gw[0], E2M1, xt_gs[0], True, True)
         nc.scalar.activation(a_sb[0][:, halves[0]], a_first[0][:], COPY)
         nc.scalar.activation(boards[0][:].indirect(l3[:, lhalves[0]]), a_sb[0][:, halves[0]], COPY)
 
-        nc.vector.tensor_copy(xt_gs[:, halves[1]], xt_plane[:].indirect(l1[:, lhalves[1]]))
-        nc.vector.tensor_copy(xt_gw[:, halves[1]], xt_tab[:].indirect(l1[:, lhalves[1]]))
+        xt_gs.append(shared.tile([P, HALF], U8, name="xt_gs1", align_bytes=64, offset=0))
+        xt_gw.append(shared.tile([P, HALF], U16, name="xt_gw1", align_bytes=64, offset=HALF))
+        nc.vector.tensor_copy(xt_gw[1][:], xt_tab[:].indirect(l1[:, lhalves[1]]))
+        nc.vector.tensor_copy(xt_gs[1][:], xt_plane[:].indirect(l1[:, lhalves[1]]))
         nc.vector.tensor_copy(a_sb[1][:, halves[0]], a_first[1][:])
         nc.scalar.activation(boards[1][:].indirect(l3[:, lhalves[0]]), a_sb[1][:, halves[0]], COPY)
         for t in range(2):
-            product(a_second[:, t, :], w_cd, E4M3, w_sc, t, xt_gw, E2M1, xt_gs, halves[1], True, True)
-        deal(w_sc[:], w_plane[:], 16, slice(2, PACK))
-        deal(w_cd[:], w_raw[:], 4, slice(2, PACK))
-        for t in range(2):
-            product(a_whole[:, t, :], w_cd, E4M3, w_sc, 2 + t, xt_gw, E2M1, xt_gs, slice(0, J), True, True)
+            product(a_second[:, t, :], w_cd, E4M3, w_sc, t, xt_gw[1], E2M1, xt_gs[1], True, True)
+        for t in range(2, PACK):
+            for h in range(2):
+                product(a_whole[:, t - 2, halves[h]], w_cd, E4M3, w_sc, t, xt_gw[h], E2M1, xt_gs[h], True, True)
         for t in range(2):
             nc.vector.tensor_copy(a_sb[t][:, halves[1]], a_second[:, t, :])
         for t in range(2):
             nc.scalar.activation(boards[t][:].indirect(l3[:, lhalves[1]]), a_sb[t][:, halves[1]], COPY)
+        boards.append(shared.tile([P, C], F32, name="board2", align_bytes=64, offset=4 * HALF))
+        boards.append(keep.tile([P, C], F32, name="board3", tag="board3", align_bytes=64))
         for t in range(2, PACK):
-            board = keep.tile([P, C], F32, name=f"board{t}", tag=f"board{t}", align_bytes=64)
-            nc.vector.memset(board[:], 0.0)
-            boards.append(board)
+            nc.gpsimd.memset(boards[t][:], 0.0)
             nc.vector.tensor_copy(a_sb[t][:], a_whole[:, t - 2, :])
             nc.scalar.activation(boards[t][:].indirect(l3[:]), a_sb[t][:], COPY)
 
@@ -163,18 +166,18 @@ def tile_list_ownthree_leaned_one_scattered_kernel(
         w0_cd = keep.tile([P, R], I32, name="w0_cd", tag="page1", align_bytes=64)
         nc.vector.tensor_copy(xo_gw[:], xo_tab[:].indirect(l2[:]))
         nc.vector.tensor_copy(xo_gs[:], xo_plane[:].indirect(l2[:]))
-        deal(w2_sc[:], late_plane[:, 0:R], 16)
+        spread_scale_rows(late_plane, late_stage)
         deal(w0_sc[:], late_plane[:, R : 2 * R], 16)
-        deal(w2_cd[:], w2_raw[:], 4)
+        deal(w2_sc[:], late_plane[:, 0:R], 16)
         deal(w0_cd[:], w0_raw[:], 4)
-        b_ps = [psum.tile([P, 2, J], F32, name=f"b_ps{u}") for u in range(2)]
+        deal(w2_cd[:], w2_raw[:], 4)
+        b_ps = [psum.tile([P, J], F32, name=f"b_ps{t}") for t in range(PACK)]
         b_sb = [keep.tile([P, J], F32, name=f"b_sb{t}") for t in range(PACK)]
         for t in range(PACK):
-            dst = b_ps[t // 2][:, t % 2, :]
-            product(dst, w2_cd, E5M2, w2_sc, t, xt_gw, E2M1, xt_gs, slice(0, J), True, False)
-            product(dst, w0_cd, E5M2, w0_sc, t, xo_gw, E4M3, xo_gs, slice(0, J), False, True)
-        for t in range(PACK):
-            nc.vector.tensor_copy(b_sb[t][:], b_ps[t // 2][:, t % 2, :])
+            product(b_ps[t][:], w0_cd, E5M2, w0_sc, t, xo_gw, E4M3, xo_gs, True, False)
+            for h in range(2):
+                product(b_ps[t][:, halves[h]], w2_cd, E5M2, w2_sc, t, xt_gw[h], E2M1, xt_gs[h], False, h == 1)
+            nc.vector.tensor_copy(b_sb[t][:], b_ps[t][:])
 
         hid = keep.tile([P, O, PACK], BF16, name="hid", align_bytes=64)
         first = keep.tile([P, PACK, O], F32, name="first")
@@ -197,13 +200,13 @@ def tile_list_ownthree_leaned_one_scattered_kernel(
 
         pages = [keep.tile([P, E], F32, name=f"page{u}", tag=f"page{u}", align_bytes=64) for u in range(2)]
         for page in pages:
-            nc.vector.memset(page[:], 0.0)
+            nc.gpsimd.memset(page[:], 0.0)
 
         hid_cd = keep.tile([P, O], U32, name="hid_cd", align_bytes=64)
         hid_sc = keep.tile([P, O], U8, name="hid_sc", align_bytes=64)
         nc.vector.quantize_mx(out=hid_cd[:].bitcast(E5M2), scales=hid_sc[:], in_=hid[:].rearrange("p o t -> p (o t)"))
 
-        p_ps = [psum.tile([P, O], F32, name=f"p_ps{u}") for u in range(2)]
+        p_ps = [psum.tile([P, O], F32, name=f"p_ps{u}", tag=f"small{u}") for u in range(2)]
         p_sb = [keep.tile([P, O], F32, name=f"p_sb{u}") for u in range(2)]
         for u in range(2):
             nc.tensor.matmul_mx(

@@ -31,7 +31,6 @@ def tile_list_ownthree_leaned_one_scattered_kernel(
     with ExitStack() as ctx:
         lists = ctx.enter_context(tc.tile_pool(name="lists", bufs=1))
         keep = ctx.enter_context(tc.tile_pool(name="keep", bufs=1))
-        shared = ctx.enter_context(tc.tile_pool(name="shared", bufs=1))
         psum = ctx.enter_context(tc.psum_pool(name="psum", bufs=1))
 
         def load_list(src, name):
@@ -49,21 +48,21 @@ def tile_list_ownthree_leaned_one_scattered_kernel(
         def load_words(queue, dst, src):
             queue.dma_start(dst.bitcast(I32), src.bitcast(I32))
 
-        def deal(dst, src, run):
+        def deal(dst, src, run, t0=0, count=PACK):
             nc.vector.tensor_copy(
-                out=dst.rearrange("p (t c i) -> p c t i", t=PACK, i=run),
-                in_=src.rearrange("p (c i t) -> p c t i", t=PACK, i=run),
+                out=dst.rearrange("p (t c i) -> p c t i", t=count, i=run),
+                in_=src.rearrange("p (c i t) -> p c t i", t=PACK, i=run)[:, :, t0 : t0 + count, :],
             )
 
         w_stage = keep.tile([4, 4, R // 4], I32, name="w_stage")
         late_stage = keep.tile([4, 4, (2 * R + N) // 4], I32, name="late_stage")
-        xt_plane = keep.tile([P, T], U8, name="xt_plane", align_bytes=64)
+        xt_plane = keep.tile([P, T], U8, name="xt_plane", tag="xt_plane", align_bytes=64)
         xo_plane = keep.tile([P, Z], U8, name="xo_plane", align_bytes=64)
         w_plane = keep.tile([P, R], U8, name="w_plane", align_bytes=64)
         late_plane = keep.tile([P, 2 * R + N], U8, name="late_plane", align_bytes=64)
-        xt_tab = keep.tile([P, T], U16, name="xt_tab", tag="board3", align_bytes=64)
+        xt_tab = keep.tile([P, T], U16, name="xt_tab", align_bytes=64)
         xo_tab = keep.tile([P, Z], U32, name="xo_tab", align_bytes=64)
-        w_raw = shared.tile([P, R], I32, name="w_raw", align_bytes=64, offset=0)
+        w_raw = keep.tile([P, R], I32, name="w_raw", align_bytes=64)
         w2_raw = keep.tile([P, R], I32, name="w2_raw", align_bytes=64)
         w0_raw = keep.tile([P, R], I32, name="w0_raw", align_bytes=64)
         wb_codes = keep.tile([P, 2 * N], U8, name="wb_codes", align_bytes=64)
@@ -84,8 +83,8 @@ def tile_list_ownthree_leaned_one_scattered_kernel(
         l1 = load_list(offs, "l1")
         load_scale_rows(nc.scalar, w_stage[:], w_scales)
         load_words(nc.sync, xt_tab[:], xt_words[0])
-        load_plane(xt_plane[:], xt_scales, (nc.scalar, nc.sync, nc.scalar, nc.sync))
         load_words(nc.scalar, w_raw[:], w_words[0].rearrange("p n t -> p (n t)"))
+        load_plane(xt_plane[:], xt_scales, (nc.scalar, nc.sync, nc.scalar, nc.sync))
         l3 = load_list(offs3, "l3")
 
         def load_weights(dst, src):
@@ -110,15 +109,15 @@ def tile_list_ownthree_leaned_one_scattered_kernel(
 
         halves = [slice(0, HALF), slice(HALF, J)]
         lhalves = [slice(0, HALF // 16), slice(HALF // 16, J // 16)]
-        w_sc = keep.tile([P, R], U8, name="w_sc", align_bytes=64)
-        w_cd = keep.tile([P, R], I32, name="w_cd", align_bytes=64)
-        xt_gs = [keep.tile([P, HALF], U8, name="xt_gs0", align_bytes=64)]
+        w_sc = [keep.tile([P, 2 * P], U8, name="w_sc0", tag="w_sc", align_bytes=64)]
+        w_cd = [keep.tile([P, 2 * P], I32, name="w_cd0", tag="w_cd", align_bytes=64)]
+        xt_gs = [keep.tile([P, HALF], U8, name=f"xt_gs{h}", align_bytes=64) for h in range(2)]
         xt_gw = [keep.tile([P, HALF], U16, name="xt_gw0", align_bytes=64)]
         spread_scale_rows(w_plane, w_stage)
-        deal(w_sc[:], w_plane[:], 16)
+        deal(w_sc[0][:], w_plane[:], 16, 0, 2)
         nc.vector.tensor_copy(xt_gw[0][:], xt_tab[:].indirect(l1[:, lhalves[0]]))
+        deal(w_cd[0][:], w_raw[:], 4, 0, 2)
         nc.vector.tensor_copy(xt_gs[0][:], xt_plane[:].indirect(l1[:, lhalves[0]]))
-        deal(w_cd[:], w_raw[:], 4)
 
         def product(dst, codes, fmt, scales, t, xw, xfmt, xs, start, stop):
             rows = slice(P * t, P * (t + 1))
@@ -127,40 +126,42 @@ def tile_list_ownthree_leaned_one_scattered_kernel(
                 rhs=xw[:].bitcast(xfmt), rhs_scale=xs[:], start=start, stop=stop,
             )
 
-        a_sb = [keep.tile([P, J], F32, name=f"a_sb{t}") for t in range(PACK)]
         a_first = [psum.tile([P, HALF], F32, name=f"a_first{t}", tag=f"small{t}") for t in range(2)]
         a_second = psum.tile([P, 2, HALF], F32, name="a_second")
-        a_whole = psum.tile([P, 2, J], F32, name="a_whole")
+        a_sb = [keep.tile([P, 2, HALF], F32, name=f"a_sb{h}", tag=f"board{2 + h}") for h in range(2)]
+        a_rest_ps = psum.tile([P, 2, J], F32, name="a_rest_ps")
+        a_rest = keep.tile([P, 2, J], F32, name="a_rest")
         for t in range(2):
-            product(a_first[t][:], w_cd, E4M3, w_sc, t, xt_gw[0], E2M1, xt_gs[0], True, True)
-        nc.scalar.activation(a_sb[0][:, halves[0]], a_first[0][:], COPY)
-        nc.scalar.activation(boards[0][:].indirect(l3[:, lhalves[0]]), a_sb[0][:, halves[0]], COPY)
+            product(a_first[t][:], w_cd[0], E4M3, w_sc[0], t, xt_gw[0], E2M1, xt_gs[0], True, True)
+        nc.scalar.activation(a_sb[0][:, 0, :], a_first[0][:], COPY)
+        nc.scalar.activation(boards[0][:].indirect(l3[:, lhalves[0]]), a_sb[0][:, 0, :], COPY)
 
-        xt_gs.append(shared.tile([P, HALF], U8, name="xt_gs1", align_bytes=64, offset=0))
-        xt_gw.append(shared.tile([P, HALF], U16, name="xt_gw1", align_bytes=64, offset=HALF))
-        nc.vector.tensor_copy(xt_gw[1][:], xt_tab[:].indirect(l1[:, lhalves[1]]))
         nc.vector.tensor_copy(xt_gs[1][:], xt_plane[:].indirect(l1[:, lhalves[1]]))
-        nc.vector.tensor_copy(a_sb[1][:, halves[0]], a_first[1][:])
-        nc.scalar.activation(boards[1][:].indirect(l3[:, lhalves[0]]), a_sb[1][:, halves[0]], COPY)
+        xt_gw.append(keep.tile([P, HALF], U16, name="xt_gw1", tag="xt_plane", align_bytes=64))
+        nc.vector.tensor_copy(xt_gw[1][:], xt_tab[:].indirect(l1[:, lhalves[1]]))
+        nc.vector.tensor_copy(a_sb[0][:, 1, :], a_first[1][:])
+        nc.scalar.activation(boards[1][:].indirect(l3[:, lhalves[0]]), a_sb[0][:, 1, :], COPY)
         for t in range(2):
-            product(a_second[:, t, :], w_cd, E4M3, w_sc, t, xt_gw[1], E2M1, xt_gs[1], True, True)
-        for t in range(2, PACK):
+            product(a_second[:, t, :], w_cd[0], E4M3, w_sc[0], t, xt_gw[1], E2M1, xt_gs[1], True, True)
+        nc.vector.tensor_copy(a_sb[1][:], a_second[:])
+        for t in range(2):
+            nc.scalar.activation(boards[t][:].indirect(l3[:, lhalves[1]]), a_sb[1][:, t, :], COPY)
+        w_sc.append(keep.tile([P, 2 * P], U8, name="w_sc1", tag="w_sc", align_bytes=64))
+        w_cd.append(keep.tile([P, 2 * P], I32, name="w_cd1", tag="w_cd", align_bytes=64))
+        deal(w_sc[1][:], w_plane[:], 16, 2, 2)
+        deal(w_cd[1][:], w_raw[:], 4, 2, 2)
+        for t in range(2):
             for h in range(2):
-                product(a_whole[:, t - 2, halves[h]], w_cd, E4M3, w_sc, t, xt_gw[h], E2M1, xt_gs[h], True, True)
-        for t in range(2):
-            nc.vector.tensor_copy(a_sb[t][:, halves[1]], a_second[:, t, :])
-        for t in range(2):
-            nc.scalar.activation(boards[t][:].indirect(l3[:, lhalves[1]]), a_sb[t][:, halves[1]], COPY)
-        boards.append(shared.tile([P, C], F32, name="board2", align_bytes=64, offset=4 * HALF))
-        boards.append(keep.tile([P, C], F32, name="board3", tag="board3", align_bytes=64))
+                product(a_rest_ps[:, t, halves[h]], w_cd[1], E4M3, w_sc[1], t, xt_gw[h], E2M1, xt_gs[h], True, True)
+        nc.vector.tensor_copy(a_rest[:], a_rest_ps[:])
         for t in range(2, PACK):
+            boards.append(keep.tile([P, C], F32, name=f"board{t}", tag=f"board{t}"))
             nc.gpsimd.memset(boards[t][:], 0.0)
-            nc.vector.tensor_copy(a_sb[t][:], a_whole[:, t - 2, :])
-            nc.scalar.activation(boards[t][:].indirect(l3[:]), a_sb[t][:], COPY)
+            nc.scalar.activation(boards[t][:].indirect(l3[:]), a_rest[:, t - 2, :], COPY)
 
         xo_gw = keep.tile([P, J], U32, name="xo_gw", align_bytes=64)
         xo_gs = keep.tile([P, J], U8, name="xo_gs", align_bytes=64)
-        w2_sc = keep.tile([P, R], U8, name="w2_sc", align_bytes=64)
+        w2_sc = keep.tile([P, R], U8, name="w2_sc", tag="larger", align_bytes=64)
         w0_sc = keep.tile([P, R], U8, name="w0_sc", align_bytes=64)
         w2_cd = keep.tile([P, R], I32, name="w2_cd", tag="page0", align_bytes=64)
         w0_cd = keep.tile([P, R], I32, name="w0_cd", tag="page1", align_bytes=64)
@@ -183,7 +184,7 @@ def tile_list_ownthree_leaned_one_scattered_kernel(
         first = keep.tile([P, PACK, O], F32, name="first")
         second = keep.tile([P, PACK, O], F32, name="second")
         third = keep.tile([P, PACK, O], F32, name="third")
-        larger = keep.tile([P, PACK, O], F32, name="larger")
+        larger = keep.tile([P, PACK, O], F32, name="larger", tag="larger", align_bytes=64)
         for t in range(PACK):
             nc.scalar.activation(first[:, t, :], boards[t][:].indirect(l4[:]), COPY, scale=sa_t[:, t : t + 1])
         for t in range(PACK):
@@ -191,12 +192,13 @@ def tile_list_ownthree_leaned_one_scattered_kernel(
         for t in range(PACK):
             nc.scalar.activation(third[:, t, :], b_sb[t][:].indirect(l6[:]), COPY, scale=sd_t[:, t : t + 1])
         nc.vector.tensor_tensor(larger[:], first[:], second[:], ALU.max)
-        nc.vector.tensor_tensor(
-            hid[:].rearrange("p (c i) t -> p c t i", i=4),
-            larger[:].rearrange("p t (c i) -> p c t i", i=4),
-            third[:].rearrange("p t (c i) -> p c t i", i=4),
-            ALU.subtract,
-        )
+        for pair in (slice(0, 2), slice(2, PACK)):
+            nc.vector.tensor_tensor(
+                hid[:].rearrange("p (c i) t -> p c t i", i=4)[:, :, pair, :],
+                larger[:].rearrange("p t (c i) -> p c t i", i=4)[:, :, pair, :],
+                third[:].rearrange("p t (c i) -> p c t i", i=4)[:, :, pair, :],
+                ALU.subtract,
+            )
 
         pages = [keep.tile([P, E], F32, name=f"page{u}", tag=f"page{u}", align_bytes=64) for u in range(2)]
         for page in pages:

@@ -58,11 +58,11 @@ def tile_list_ownthree_leaned_one_scattered_kernel(
         late_stage = keep.tile([4, 4, (2 * R + N) // 4], I32, name="late_stage")
         xt_plane = keep.tile([P, T], U8, name="xt_plane", tag="xt_plane", align_bytes=64)
         xo_plane = keep.tile([P, Z], U8, name="xo_plane", align_bytes=64)
-        w_plane = keep.tile([P, R], U8, name="w_plane", align_bytes=64)
+        w_plane = keep.tile([P, R], U8, name="w_plane", tag="board2", align_bytes=64)
         late_plane = keep.tile([P, 2 * R + N], U8, name="late_plane", align_bytes=64)
         xt_tab = keep.tile([P, T], U16, name="xt_tab", align_bytes=64)
         xo_tab = keep.tile([P, Z], U32, name="xo_tab", align_bytes=64)
-        w_raw = keep.tile([P, R], I32, name="w_raw", align_bytes=64)
+        w_raw = keep.tile([P, R], I32, name="w_raw", tag="board3", align_bytes=64)
         w2_raw = keep.tile([P, R], I32, name="w2_raw", align_bytes=64)
         w0_raw = keep.tile([P, R], I32, name="w0_raw", align_bytes=64)
         wb_codes = keep.tile([P, 2 * N], U8, name="wb_codes", align_bytes=64)
@@ -93,10 +93,10 @@ def tile_list_ownthree_leaned_one_scattered_kernel(
         l2 = load_list(offs2, "l2")
         load_words(nc.sync, xo_tab[:], xo_words[0].rearrange("p n t -> p (n t)"))
         load_plane(xo_plane[:], xo_scales)
+        load_words(nc.sync, w0_raw[:], w0_words[0].rearrange("p n t -> p (n t)"))
         load_scale_rows(nc.sync, late_stage[:, :, 0 : R // 4], w2_scales)
         load_scale_rows(nc.sync, late_stage[:, :, R // 4 : 2 * R // 4], w0_scales)
         load_scale_rows(nc.sync, late_stage[:, :, 2 * R // 4 :], wb_scales)
-        load_words(nc.sync, w0_raw[:], w0_words[0].rearrange("p n t -> p (n t)"))
         load_words(nc.sync, w2_raw[:], w2_words[0].rearrange("p n t -> p (n t)"))
         l4 = load_list(offs4, "l4")
         load_weights(sa_t, sa)
@@ -128,9 +128,8 @@ def tile_list_ownthree_leaned_one_scattered_kernel(
 
         a_first = [psum.tile([P, HALF], F32, name=f"a_first{t}", tag=f"small{t}") for t in range(2)]
         a_second = psum.tile([P, 2, HALF], F32, name="a_second")
-        a_sb = [keep.tile([P, 2, HALF], F32, name=f"a_sb{h}", tag=f"board{2 + h}") for h in range(2)]
+        a_sb = [keep.tile([P, 2, HALF], F32, name=f"a_sb{h}", tag=f"a_sb{h}") for h in range(2)]
         a_rest_ps = psum.tile([P, 2, J], F32, name="a_rest_ps")
-        a_rest = keep.tile([P, 2, J], F32, name="a_rest")
         for t in range(2):
             product(a_first[t][:], w_cd[0], E4M3, w_sc[0], t, xt_gw[0], E2M1, xt_gs[0], True, True)
         nc.scalar.activation(a_sb[0][:, 0, :], a_first[0][:], COPY)
@@ -153,10 +152,12 @@ def tile_list_ownthree_leaned_one_scattered_kernel(
         for t in range(2):
             for h in range(2):
                 product(a_rest_ps[:, t, halves[h]], w_cd[1], E4M3, w_sc[1], t, xt_gw[h], E2M1, xt_gs[h], True, True)
+        for t in range(2, PACK):
+            boards.append(keep.tile([P, C], F32, name=f"board{t}", tag=f"board{t}", align_bytes=64))
+            nc.vector.memset(boards[t][:], 0.0)
+        a_rest = keep.tile([P, 2, J], F32, name="a_rest", tag="a_sb0")
         nc.vector.tensor_copy(a_rest[:], a_rest_ps[:])
         for t in range(2, PACK):
-            boards.append(keep.tile([P, C], F32, name=f"board{t}", tag=f"board{t}"))
-            nc.gpsimd.memset(boards[t][:], 0.0)
             nc.scalar.activation(boards[t][:].indirect(l3[:]), a_rest[:, t - 2, :], COPY)
 
         xo_gw = keep.tile([P, J], U32, name="xo_gw", align_bytes=64)
@@ -167,10 +168,10 @@ def tile_list_ownthree_leaned_one_scattered_kernel(
         w0_cd = keep.tile([P, R], I32, name="w0_cd", tag="page1", align_bytes=64)
         nc.vector.tensor_copy(xo_gw[:], xo_tab[:].indirect(l2[:]))
         nc.vector.tensor_copy(xo_gs[:], xo_plane[:].indirect(l2[:]))
+        deal(w0_cd[:], w0_raw[:], 4)
         spread_scale_rows(late_plane, late_stage)
         deal(w0_sc[:], late_plane[:, R : 2 * R], 16)
         deal(w2_sc[:], late_plane[:, 0:R], 16)
-        deal(w0_cd[:], w0_raw[:], 4)
         deal(w2_cd[:], w2_raw[:], 4)
         b_ps = [psum.tile([P, J], F32, name=f"b_ps{t}") for t in range(PACK)]
         b_sb = [keep.tile([P, J], F32, name=f"b_sb{t}") for t in range(PACK)]

from contextlib import ExitStack

import concourse.mybir as mybir

F32 = mybir.dt.float32
BF16 = mybir.dt.bfloat16
I32 = mybir.dt.int32
U32 = mybir.dt.uint32
U16 = mybir.dt.uint16
U8 = mybir.dt.uint8
E4M3 = mybir.dt.float8_e4m3fn_x4
E5M2 = mybir.dt.float8_e5m2_x4
E2M1 = mybir.dt.float4_e2m1fn_x4
COPY = mybir.ActivationFunctionType.Copy
ALU = mybir.AluOpType

P = 128
PACK = 4
T, J, R, Z, C, O, N, E = 1024, 256, 512, 1024, 512, 128, 256, 1024
HALF = J // 2

FLOPS = 2 * 512 * R * J * 3 + 2 * R * N * O


def tile_list_ownthree_leaned_one_scattered_kernel(
    tc, xt_words, xt_scales, xo_words, xo_scales, w_words, w_scales, w2_words, w2_scales,
    w0_words, w0_scales, sa, sb, sd, wb_words, wb_scales,
    offs, offs2, offs3, offs4, offs5, offs6, offs7, out,
):
    nc = tc.nc
    with ExitStack() as ctx:
        lists = ctx.enter_context(tc.tile_pool(name="lists", bufs=1))
        keep = ctx.enter_context(tc.tile_pool(name="keep", bufs=1))
        psum = ctx.enter_context(tc.psum_pool(name="psum", bufs=1))

        def load_list(src, name):
            tile = lists.tile(list(src.shape), U16, name=name)
            nc.sync.dma_start(tile[:], src)
            return tile

        def load_scale_rows(queue, dst, src):
            queue.dma_start(dst, src[0].bitcast(I32).rearrange("(q r) n -> r q n", r=4))

        def spread_scale_rows(plane, staged):
            for q in range(4):
                nc.vector.tensor_copy(out=plane[32 * q : 32 * q + 4, :].bitcast(I32), in_=staged[:, q, :])

        def load_words(queue, dst, src):
            queue.dma_start(dst.bitcast(I32), src.bitcast(I32))

        def deal(dst, src, run, t0=0, count=PACK):
            nc.vector.tensor_copy(
                out=dst.rearrange("p (t c i) -> p c t i", t=count, i=run),
                in_=src.rearrange("p (c i t) -> p c t i", t=PACK, i=run)[:, :, t0 : t0 + count, :],
            )

        w_stage = keep.tile([4, 4, R // 4], I32, name="w_stage")
        late_stage = keep.tile([4, 4, (2 * R + N) // 4], I32, name="late_stage")
        xt_plane = keep.tile([P, T], U8, name="xt_plane", tag="xt_plane", align_bytes=64)
        xo_plane = keep.tile([P, Z], U8, name="xo_plane", align_bytes=64)
        w_plane = keep.tile([P, R], U8, name="w_plane", tag="board2", align_bytes=64)
        late_plane = keep.tile([P, 2 * R + N], U8, name="late_plane", align_bytes=64)
        xt_tab = keep.tile([P, T], U16, name="xt_tab", align_bytes=64)
        xo_tab = keep.tile([P, Z], U32, name="xo_tab", align_bytes=64)
        w_raw = keep.tile([P, R], I32, name="w_raw", tag="board3", align_bytes=64)
        w2_raw = keep.tile([P, R], I32, name="w2_raw", align_bytes=64)
        w0_raw = keep.tile([P, R], I32, name="w0_raw", align_bytes=64)
        wb_codes = keep.tile([P, 2 * N], U8, name="wb_codes", align_bytes=64)
        sa_t = keep.tile([P, PACK], F32, name="sa_t")
        sb_t = keep.tile([P, PACK], F32, name="sb_t")
        sd_t = keep.tile([P, PACK], F32, name="sd_t")

        boards = [keep.tile([P, C], F32, name=f"board{t}") for t in range(2)]
        for plane in (xt_plane, w_plane, xo_plane, late_plane):
            nc.vector.memset(plane[:].bitcast(I32), 0)
        for board in boards:
            nc.vector.memset(board[:], 0.0)

        def load_plane(dst, src, queues=(nc.sync,) * 4):
            for q in range(4):
                queues[q].dma_start(dst[32 * q : 32 * q + 4, :].bitcast(I32), src[0, 4 * q : 4 * q + 4, :].bitcast(I32))

        l1 = load_list(offs, "l1")
        load_scale_rows(nc.scalar, w_stage[:], w_scales)
        load_words(nc.sync, xt_tab[:], xt_words[0])
        load_words(nc.scalar, w_raw[:], w_words[0].rearrange("p n t -> p (n t)"))
        load_plane(xt_plane[:], xt_scales, (nc.scalar, nc.sync, nc.scalar, nc.sync))
        l3 = load_list(offs3, "l3")

        def load_weights(dst, src):
            nc.sync.dma_start(dst[:], src.rearrange("(p t) one -> p (t one)", t=PACK))

        l2 = load_list(offs2, "l2")
        load_words(nc.sync, xo_tab[:], xo_words[0].rearrange("p n t -> p (n t)"))
        load_plane(xo_plane[:], xo_scales)
        load_words(nc.sync, w0_raw[:], w0_words[0].rearrange("p n t -> p (n t)"))
        load_scale_rows(nc.sync, late_stage[:, :, 0 : R // 4], w2_scales)
        load_scale_rows(nc.sync, late_stage[:, :, R // 4 : 2 * R // 4], w0_scales)
        load_scale_rows(nc.sync, late_stage[:, :, 2 * R // 4 :], wb_scales)
        load_words(nc.sync, w2_raw[:], w2_words[0].rearrange("p n t -> p (n t)"))
        l4 = load_list(offs4, "l4")
        load_weights(sa_t, sa)
        l5 = load_list(offs5, "l5")
        load_weights(sb_t, sb)
        l6 = load_list(offs6, "l6")
        load_weights(sd_t, sd)
        load_words(nc.sync, wb_codes[:], wb_words[0])
        l7 = load_list(offs7, "l7")

        halves = [slice(0, HALF), slice(HALF, J)]
        lhalves = [slice(0, HALF // 16), slice(HALF // 16, J // 16)]
        w_sc = [keep.tile([P, 2 * P], U8, name="w_sc0", tag="w_sc", align_bytes=64)]
        w_cd = [keep.tile([P, 2 * P], I32, name="w_cd0", tag="w_cd", align_bytes=64)]
        xt_gs = [keep.tile([P, HALF], U8, name=f"xt_gs{h}", align_bytes=64) for h in range(2)]
        xt_gw = [keep.tile([P, HALF], U16, name="xt_gw0", align_bytes=64)]
        spread_scale_rows(w_plane, w_stage)
        deal(w_sc[0][:], w_plane[:], 16, 0, 2)
        nc.vector.tensor_copy(xt_gw[0][:], xt_tab[:].indirect(l1[:, lhalves[0]]))
        deal(w_cd[0][:], w_raw[:], 4, 0, 2)
        nc.vector.tensor_copy(xt_gs[0][:], xt_plane[:].indirect(l1[:, lhalves[0]]))

        def product(dst, codes, fmt, scales, t, xw, xfmt, xs, start, stop):
            rows = slice(P * t, P * (t + 1))
            nc.tensor.matmul_mx(
                out=dst, lhsT=codes[:, rows].bitcast(fmt), lhsT_scale=scales[:, rows],
                rhs=xw[:].bitcast(xfmt), rhs_scale=xs[:], start=start, stop=stop,
            )

        a_first = [psum.tile([P, HALF], F32, name=f"a_first{t}", tag=f"small{t}") for t in range(2)]
        a_second = psum.tile([P, 2, HALF], F32, name="a_second")
        a_sb = [keep.tile([P, 2, HALF], F32, name=f"a_sb{h}", tag=f"a_sb{h}") for h in range(2)]
        a_rest_ps = psum.tile([P, 2, J], F32, name="a_rest_ps")
        for t in range(2):
            product(a_first[t][:], w_cd[0], E4M3, w_sc[0], t, xt_gw[0], E2M1, xt_gs[0], True, True)
        nc.scalar.activation(a_sb[0][:, 0, :], a_first[0][:], COPY)
        nc.scalar.activation(boards[0][:].indirect(l3[:, lhalves[0]]), a_sb[0][:, 0, :], COPY)

        nc.vector.tensor_copy(xt_gs[1][:], xt_plane[:].indirect(l1[:, lhalves[1]]))
        xt_gw.append(keep.tile([P, HALF], U16, name="xt_gw1", tag="xt_plane", align_bytes=64))
        nc.vector.tensor_copy(xt_gw[1][:], xt_tab[:].indirect(l1[:, lhalves[1]]))
        nc.vector.tensor_copy(a_sb[0][:, 1, :], a_first[1][:])
        nc.scalar.activation(boards[1][:].indirect(l3[:, lhalves[0]]), a_sb[0][:, 1, :], COPY)
        for t in range(2):
            product(a_second[:, t, :], w_cd[0], E4M3, w_sc[0], t, xt_gw[1], E2M1, xt_gs[1], True, True)
        nc.vector.tensor_copy(a_sb[1][:], a_second[:])
        for t in range(2):
            nc.scalar.activation(boards[t][:].indirect(l3[:, lhalves[1]]), a_sb[1][:, t, :], COPY)
        w_sc.append(keep.tile([P, 2 * P], U8, name="w_sc1", tag="w_sc", align_bytes=64))
        w_cd.append(keep.tile([P, 2 * P], I32, name="w_cd1", tag="w_cd", align_bytes=64))
        deal(w_sc[1][:], w_plane[:], 16, 2, 2)
        deal(w_cd[1][:], w_raw[:], 4, 2, 2)
        for t in range(2):
            for h in range(2):
                product(a_rest_ps[:, t, halves[h]], w_cd[1], E4M3, w_sc[1], t, xt_gw[h], E2M1, xt_gs[h], True, True)
        for t in range(2, PACK):
            boards.append(keep.tile([P, C], F32, name=f"board{t}", tag=f"board{t}", align_bytes=64))
            nc.vector.memset(boards[t][:], 0.0)
        a_rest = keep.tile([P, 2, J], F32, name="a_rest", tag="a_sb0")
        nc.vector.tensor_copy(a_rest[:], a_rest_ps[:])
        for t in range(2, PACK):
            nc.scalar.activation(boards[t][:].indirect(l3[:]), a_rest[:, t - 2, :], COPY)

        xo_gw = keep.tile([P, J], U32, name="xo_gw", align_bytes=64)
        xo_gs = keep.tile([P, J], U8, name="xo_gs", align_bytes=64)
        w2_sc = keep.tile([P, R], U8, name="w2_sc", tag="larger", align_bytes=64)
        w0_sc = keep.tile([P, R], U8, name="w0_sc", align_bytes=64)
        w2_cd = keep.tile([P, R], I32, name="w2_cd", tag="page0", align_bytes=64)
        w0_cd = keep.tile([P, R], I32, name="w0_cd", tag="page1", align_bytes=64)
        nc.vector.tensor_copy(xo_gw[:], xo_tab[:].indirect(l2[:]))
        nc.vector.tensor_copy(xo_gs[:], xo_plane[:].indirect(l2[:]))
        deal(w0_cd[:], w0_raw[:], 4)
        spread_scale_rows(late_plane, late_stage)
        deal(w0_sc[:], late_plane[:, R : 2 * R], 16)
        deal(w2_sc[:], late_plane[:, 0:R], 16)
        deal(w2_cd[:], w2_raw[:], 4)
        b_ps = [psum.tile([P, J], F32, name=f"b_ps{t}") for t in range(PACK)]
        b_sb = [keep.tile([P, J], F32, name=f"b_sb{t}") for t in range(PACK)]
        for t in range(PACK):
            product(b_ps[t][:], w0_cd, E5M2, w0_sc, t, xo_gw, E4M3, xo_gs, True, False)
            for h in range(2):
                product(b_ps[t][:, halves[h]], w2_cd, E5M2, w2_sc, t, xt_gw[h], E2M1, xt_gs[h], False, h == 1)
            nc.vector.tensor_copy(b_sb[t][:], b_ps[t][:])

        hid = keep.tile([P, O, PACK], BF16, name="hid", align_bytes=64)
        first = keep.tile([P, PACK, O], F32, name="first")
        second = keep.tile([P, PACK, O], F32, name="second")
        third = keep.tile([P, PACK, O], F32, name="third")
        larger = keep.tile([P, PACK, O], F32, name="larger", tag="larger", align_bytes=64)
        for t in range(PACK):
            nc.scalar.activation(first[:, t, :], boards[t][:].indirect(l4[:]), COPY, scale=sa_t[:, t : t + 1])
        for t in range(PACK):
            nc.scalar.activation(second[:, t, :], boards[t][:].indirect(l5[:]), COPY, scale=sb_t[:, t : t + 1])
        for t in range(PACK):
            nc.scalar.activation(third[:, t, :], b_sb[t][:].indirect(l6[:]), COPY, scale=sd_t[:, t : t + 1])
        nc.vector.tensor_tensor(larger[:], first[:], second[:], ALU.max)
        for pair in (slice(0, 2), slice(2, PACK)):
            nc.vector.tensor_tensor(
                hid[:].rearrange("p (c i) t -> p c t i", i=4)[:, :, pair, :],
                larger[:].rearrange("p t (c i) -> p c t i", i=4)[:, :, pair, :],
                third[:].rearrange("p t (c i) -> p c t i", i=4)[:, :, pair, :],
                ALU.subtract,
            )

        pages = [keep.tile([P, E], F32, name=f"page{u}", tag=f"page{u}", align_bytes=64) for u in range(2)]
        for page in pages:
            nc.gpsimd.memset(page[:], 0.0)

        hid_cd = keep.tile([P, O], U32, name="hid_cd", align_bytes=64)
        hid_sc = keep.tile([P, O], U8, name="hid_sc", align_bytes=64)
        nc.vector.quantize_mx(out=hid_cd[:].bitcast(E5M2), scales=hid_sc[:], in_=hid[:].rearrange("p o t -> p (o t)"))

        p_ps = [psum.tile([P, O], F32, name=f"p_ps{u}", tag=f"small{u}") for u in range(2)]
        p_sb = [keep.tile([P, O], F32, name=f"p_sb{u}") for u in range(2)]
        for u in range(2):
            nc.tensor.matmul_mx(
                out=p_ps[u][:],
                lhsT=wb_codes[:, 2 * P * u : 2 * P * (u + 1)].bitcast(E2M1),
                lhsT_scale=late_plane[:, 2 * R + P * u : 2 * R + P * (u + 1)],
                rhs=hid_cd[:].bitcast(E5M2), rhs_scale=hid_sc[:], start=True, stop=True,
            )
        nc.vector.tensor_copy(p_sb[0][:], p_ps[0][:])
        nc.vector.tensor_copy(pages[0][:].indirect(l7[:]), p_sb[0][:])
        nc.sync.dma_start(out[0:P, :], pages[0][:])
        nc.scalar.activation(p_sb[1][:], p_ps[1][:], COPY)
        nc.scalar.activation(pages[1][:].indirect(l7[:]), p_sb[1][:], COPY)
        nc.scalar.dma_start(out[P : 2 * P, :], pages[1][:])
